import numpy as np
import ml_dtypes


def mxq(x, axis, fmt="e4m3"):
    dtype, down = {"e4m3": (ml_dtypes.float8_e4m3fn, 7), "e5m2": (ml_dtypes.float8_e5m2, 14)}[fmt]
    v = np.moveaxis(np.asarray(x, np.float32).astype(ml_dtypes.bfloat16).astype(np.float64), axis, -1)
    blocks = v.reshape(v.shape[:-1] + (-1, 32))
    amax = np.abs(blocks).max(-1, keepdims=True)
    byte = np.maximum(np.where(amax > 0, np.frexp(amax)[1] - 1 + 127, 0) - down, 1)
    scale = np.exp2(byte - 127.0)
    codes = (blocks / scale).astype(np.float32).astype(dtype).astype(np.float64)
    return np.moveaxis((codes * scale).reshape(v.shape), -1, axis)


WIDE = False


def mx_kscale(k):
    if not WIDE:
        return np.ones(k)
    levels = np.array([30, -30])
    if k % 512:
        return np.exp2(np.random.permutation(np.resize(levels, k // 32))).repeat(32)
    a = np.empty((k // 512, 16))
    for p in range(k // 512):
        a[p, :8] = np.random.permutation(np.resize(levels, 8))
        for g in range(8):
            far = levels[np.abs(levels - a[p, g]) >= 10]
            a[p, g + 8] = far[np.random.randint(len(far))]
    return np.exp2(a.ravel()).repeat(32)


def f64(x):
    return np.asarray(x).astype(np.float64)


def striped(idx):
    return np.tile(np.asarray(idx).reshape(-1, 16).T, (8, 1)).astype(np.uint16)


def unstriped(offs):
    return offs[:16].T.reshape(-1).astype(np.int64)


E2M1 = np.array([0.0, 0.5, 1.0, 1.5, 2.0, 3.0, 4.0, 6.0, -0.0, -0.5, -1.0, -1.5, -2.0, -3.0, -4.0, -6.0])


def pack_weight(w, fmt):
    k, n = w.shape
    w = f64(np.asarray(w, np.float32).astype(ml_dtypes.bfloat16)).reshape(k // 32, 32, n)
    amax = np.abs(w).max(1)
    if fmt in ("e4m3", "e5m2"):
        byte = np.frexp(amax)[1] - 1 + 127 - (7 if fmt == "e4m3" else 14)
    else:
        mant, ex = np.frexp(amax / 6.0)
        byte = np.where(mant > 0.5, ex, ex - 1) + 127
    byte = np.clip(np.where(amax > 0, byte, 1), 1, 254)
    scaled = (w * np.exp2(127.0 - byte)[:, None, :]).reshape(k, n).astype(np.float32)
    by_word = np.ascontiguousarray(scaled.reshape(k // 512, 128, 4, n).transpose(0, 1, 3, 2))
    if fmt in ("e4m3", "e5m2"):
        words = by_word.astype(ml_dtypes.float8_e4m3fn if fmt == "e4m3" else ml_dtypes.float8_e5m2).view(np.uint8)
    else:
        c = by_word.astype(ml_dtypes.float4_e2m1fn).view(np.uint8) & 0xF
        words = (c[..., 0::2] | (c[..., 1::2] << 4)).reshape(k // 512, 128, 2 * n)
    return np.ascontiguousarray(words), np.ascontiguousarray(byte.astype(np.uint8).reshape(k // 512, 16, n))


def unpack_weight(words, scales, fmt):
    g, _, n = scales.shape
    words = np.ascontiguousarray(words).reshape(g, 128, n, -1)
    if fmt in ("e4m3", "e5m2"):
        vals = words.view(ml_dtypes.float8_e4m3fn if fmt == "e4m3" else ml_dtypes.float8_e5m2).astype(np.float64)
    else:
        nib = np.empty((g, 128, n, 4), np.uint8)
        nib[..., 0::2] = words & 0xF
        nib[..., 1::2] = words >> 4
        vals = E2M1[nib]
    vals = vals * np.repeat(np.exp2(scales.astype(np.float64) - 127.0), 8, axis=1)[..., None]
    return vals.transpose(0, 1, 3, 2).reshape(g * 512, n)


def sigmoid(v):
    return 1.0 / (1.0 + np.exp(-v))


K, T, J, R, Q, O, N = 512, 1024, 256, 512, 1024, 256, 256


def setup_inputs():
    n = np.random.standard_normal
    idx = np.random.permutation(T)[:J]
    idx2 = np.random.permutation(J)[:O]
    idx3 = np.random.permutation(Q)[:O]
    idx4 = np.random.permutation(J)[:O]
    idx5 = np.random.permutation(Q)[:O]
    idx6 = np.random.permutation(T)[:O]
    fk = mx_kscale(K)
    fr = mx_kscale(R)
    xtp = pack_weight(n((K, T)) / fk[:, None], "e5m2")
    wp = pack_weight(n((K, R)) * 1 / np.sqrt(K) * fk[:, None] * fr, "e2m1")
    w2p = pack_weight(n((K, R)) * 1 / np.sqrt(K) * fk[:, None] * fr, "e4m3")
    wbp = pack_weight(n((R, N)) * 1 / np.sqrt(R) / fr[:, None], "e2m1")
    wsp = pack_weight(n((K, N)) * 1 / np.sqrt(K) * fk[:, None], "e2m1")
    return {
        "xt_words": xtp[0],
        "xt_scales": xtp[1],
        "w_words": wp[0],
        "w_scales": wp[1],
        "w2_words": w2p[0],
        "w2_scales": w2p[1],
        "tg": (1.0 * n((R, Q))).astype(np.float32),
        "sg": (np.random.uniform(0.6, 1.6, (R, 1))).astype(np.float32),
        "bg": (np.random.uniform(-1.0, 1.0, (R, 1))).astype(np.float32),
        "sh": (np.random.uniform(0.6, 1.6, (R, 1))).astype(np.float32),
        "wb_words": wbp[0],
        "wb_scales": wbp[1],
        "ws_words": wsp[0],
        "ws_scales": wsp[1],
        "offs": striped(idx),
        "offs2": striped(idx2),
        "offs3": striped(idx3),
        "offs4": striped(idx4),
        "offs5": striped(idx5),
        "offs6": striped(idx6),
    }


def reference(xt_words, xt_scales, w_words, w_scales, w2_words, w2_scales, tg, sg, bg, sh, wb_words, wb_scales, ws_words, ws_scales, offs, offs2, offs3, offs4, offs5, offs6):
    idx = unstriped(offs)
    idx2 = unstriped(offs2)
    idx3 = unstriped(offs3)
    idx4 = unstriped(offs4)
    idx5 = unstriped(offs5)
    idx6 = unstriped(offs6)
    xtu = unpack_weight(xt_words, xt_scales, "e5m2")
    wu = unpack_weight(w_words, w_scales, "e2m1")
    w2u = unpack_weight(w2_words, w2_scales, "e4m3")
    wbu = unpack_weight(wb_words, wb_scales, "e2m1")
    wsu = unpack_weight(ws_words, ws_scales, "e2m1")
    xtidxg = xtu[:, idx]
    a = wu.T @ xtidxg
    b = w2u.T @ xtidxg
    u1 = a[:, idx2] * sigmoid(f64(tg)[:, idx3] * f64(sg) + f64(bg))
    u2 = b[:, idx4] * sigmoid(f64(tg)[:, idx5] * f64(sh))
    hid = np.maximum(u1, u2)
    hidq = mxq(hid, 0, "e4m3")
    xtidx6g = xtu[:, idx6]
    y = wbu.T @ hidq + wsu.T @ xtidx6g
    return y

@@ -1,0 +1,161 @@
+from contextlib import ExitStack
+
+import concourse.mybir as mybir
+
+K, T, J, R, Q, O, N = 512, 1024, 256, 512, 1024, 256, 256
+FLOPS = 2 * K * R * J * 2 + 2 * R * N * O + 2 * K * N * O
+
+F32 = mybir.dt.float32
+BF16 = mybir.dt.bfloat16
+I32 = mybir.dt.int32
+U32 = mybir.dt.uint32
+U16 = mybir.dt.uint16
+U8 = mybir.dt.uint8
+E4M3 = mybir.dt.float8_e4m3fn_x4
+E5M2 = mybir.dt.float8_e5m2_x4
+E2M1 = mybir.dt.float4_e2m1fn_x4
+MULT = mybir.AluOpType.mult
+MAX = mybir.AluOpType.max
+SIGMOID = mybir.ActivationFunctionType.Sigmoid
+
+P = 128
+PACK = 4
+SPARE = 8
+
+
+def tile_list_twogates_twow_further_plain_kernel(
+    tc, xt_words, xt_scales, w_words, w_scales, w2_words, w2_scales, tg, sg, bg, sh,
+    wb_words, wb_scales, ws_words, ws_scales, offs, offs2, offs3, offs4, offs5, offs6, out,
+):
+    nc = tc.nc
+    with ExitStack() as ctx:
+        lists = ctx.enter_context(tc.tile_pool(name="lists", bufs=1))
+        keep = ctx.enter_context(tc.tile_pool(name="keep", bufs=1))
+        psum = ctx.enter_context(tc.psum_pool(name="psum", bufs=8))
+
+        def load_list(src, name):
+            tile = lists.tile([P, 16], U16, name=name)
+            nc.sync.dma_start(tile[:], src)
+            return tile
+
+        def load_plane(eng, plane, src):
+            rows = src[0].bitcast(I32)
+            for quad in range(4):
+                four = rows[4 * quad : 4 * quad + 4, :]
+                eng.dma_start(plane[32 * quad : 32 * quad + 32, :].bitcast(I32), four.unsqueeze(0).to_broadcast([8, 4, rows.shape[1]]))
+
+        xt_plane = keep.tile([P, T], U8, align_bytes=64)
+        w_plane_raw = keep.tile([P, R], U8, align_bytes=64)
+        w2_plane_raw = keep.tile([P, R], U8, align_bytes=64)
+        wb_plane = keep.tile([P, N], U8, align_bytes=64)
+        ws_plane = keep.tile([P, N], U8, align_bytes=64)
+
+        sg_t = keep.tile([P, PACK], F32)
+        bg_t = keep.tile([P, PACK], F32)
+        sh_t = keep.tile([P, PACK], F32)
+        for tile, src in ((sg_t, sg), (bg_t, bg), (sh_t, sh)):
+            nc.gpsimd.dma_start(tile[:], src.rearrange("(p t) one -> p (t one)", t=PACK))
+
+        l1 = load_list(offs, "l1")
+        xt_codes = keep.tile([P, T], U32, align_bytes=64)
+        nc.sync.dma_start(xt_codes[:].bitcast(I32), xt_words[0].rearrange("p c r -> p (c r)").bitcast(I32))
+        load_plane(nc.scalar, xt_plane, xt_scales)
+        l6 = load_list(offs6, "l6")
+        tg_rows = tg.rearrange("(p t) q -> p t q", t=PACK)
+        tg_t = [keep.tile([P, Q], F32, name="tg%d" % t) for t in range(PACK)]
+        nc.sync.dma_start(tg_t[0][:], tg_rows[:, 0, :])
+
+        l3 = load_list(offs3, "l3")
+        w_raw = keep.tile([P, R], U16, align_bytes=64)
+        nc.sync.dma_start(w_raw[:].bitcast(I32), w_words[0].bitcast(I32))
+        load_plane(nc.sync, w_plane_raw, w_scales)
+        l5 = load_list(offs5, "l5")
+        nc.sync.dma_start(tg_t[1][:], tg_rows[:, 1, :])
+
+        l2 = load_list(offs2, "l2")
+        w2_raw = keep.tile([P, R], U32, align_bytes=64)
+        nc.sync.dma_start(w2_raw[:].bitcast(I32), w2_words[0].rearrange("p c r -> p (c r)").bitcast(I32))
+        load_plane(nc.sync, w2_plane_raw, w2_scales)
+        nc.sync.dma_start(tg_t[2][:], tg_rows[:, 2, :])
+        nc.sync.dma_start(tg_t[3][:], tg_rows[:, 3, :])
+        l4 = load_list(offs4, "l4")
+        ws_codes = keep.tile([P, N], U16, align_bytes=64)
+        nc.sync.dma_start(ws_codes[:].bitcast(I32), ws_words[0].bitcast(I32))
+        load_plane(nc.sync, ws_plane, ws_scales)
+        wb_codes = keep.tile([P, N], U16, align_bytes=64)
+        nc.sync.dma_start(wb_codes[:].bitcast(I32), wb_words[0].bitcast(I32))
+        load_plane(nc.sync, wb_plane, wb_scales)
+
+        a_win = [keep.tile([P, J + SPARE], F32, name="a%d" % t) for t in range(PACK)]
+        b_win = [keep.tile([P, J + SPARE], F32, name="b%d" % t) for t in range(PACK)]
+        for t in range(PACK):
+            nc.gpsimd.memset(a_win[t][:, J:], 0.0)
+            nc.gpsimd.memset(b_win[t][:, J:], 0.0)
+
+        def dealt(raw):
+            return raw[:].rearrange("p (m t) -> p t m", t=PACK)
+
+        x1_plane = keep.tile([P, J], U8, align_bytes=64)
+        nc.vector.tensor_copy(x1_plane[:], xt_plane[:].indirect(l1[:]))
+        x1_codes = keep.tile([P, J], U32, align_bytes=64)
+        nc.vector.tensor_copy(x1_codes[:], xt_codes[:].indirect(l1[:]))
+        x6_plane = keep.tile([P, O], U8, align_bytes=64)
+        nc.vector.tensor_copy(x6_plane[:], xt_plane[:].indirect(l6[:]))
+        x6_codes = keep.tile([P, O], U32, align_bytes=64)
+        nc.vector.tensor_copy(x6_codes[:], xt_codes[:].indirect(l6[:]))
+        w_codes = keep.tile([P, PACK, P], U16, align_bytes=64)
+        nc.scalar.copy(w_codes[:], dealt(w_raw))
+        w_plane = keep.tile([P, PACK, P], U8, align_bytes=64)
+        nc.vector.tensor_copy(w_plane[:], dealt(w_plane_raw))
+        w2_codes = keep.tile([P, PACK, P], U32, align_bytes=64)
+        nc.vector.tensor_copy(w2_codes[:], dealt(w2_raw))
+        w2_plane = keep.tile([P, PACK, P], U8, align_bytes=64)
+        nc.vector.tensor_copy(w2_plane[:], dealt(w2_plane_raw))
+
+
+        def first_stage(codes, fmt, plane, t):
+            acc = psum.tile([P, J], F32, name="acc")
+            nc.tensor.matmul_mx(acc[:], lhsT=codes[:, t, :].bitcast(fmt), lhsT_scale=plane[:, t, :],
+                                rhs=x1_codes[:].bitcast(E5M2), rhs_scale=x1_plane[:], start=True, stop=True)
+            return acc
+
+        a_acc = [first_stage(w_codes, E2M1, w_plane, t) for t in range(PACK)]
+        b_acc = [first_stage(w2_codes, E4M3, w2_plane, t) for t in range(PACK)]
+
+        u1 = keep.tile([P, PACK, O], F32)
+        u2 = keep.tile([P, PACK, O], F32)
+        for t in range(PACK):
+            g1 = keep.tile([P, O], F32, name="g1_%d" % t)
+            nc.scalar.activation(g1[:], tg_t[t][:].indirect(l3[:]), SIGMOID, bias=bg_t[:, t : t + 1], scale=sg_t[:, t : t + 1])
+            nc.vector.tensor_copy(a_win[t][:, :J], a_acc[t][:])
+            nc.vector.tensor_tensor(u1[:, t, :], a_win[t][:].indirect(l2[:]), g1[:], MULT)
+            g2 = keep.tile([P, O], F32, name="g2_%d" % t)
+            nc.scalar.activation(g2[:], tg_t[t][:].indirect(l5[:]), SIGMOID, scale=sh_t[:, t : t + 1])
+            nc.scalar.copy(b_win[t][:, :J], b_acc[t][:])
+            nc.vector.tensor_tensor(u2[:, t, :], b_win[t][:].indirect(l4[:]), g2[:], MULT)
+
+        hid = keep.tile([P, O, PACK], BF16, align_bytes=64)
+        nc.vector.tensor_tensor(
+            hid[:].rearrange("p (c i) t -> p c t i", i=4),
+            u1[:].rearrange("p t (c i) -> p c t i", i=4),
+            u2[:].rearrange("p t (c i) -> p c t i", i=4),
+            MAX,
+        )
+        hid_codes = keep.tile([P, O], U32, align_bytes=64)
+        hid_plane = keep.tile([P, O], U8, align_bytes=64)
+        nc.vector.quantize_mx(out=hid_codes[:].bitcast(E4M3), scales=hid_plane[:], in_=hid[:].rearrange("p o t -> p (o t)"))
+
+        for half in range(N // P):
+            cols = slice(half * P, (half + 1) * P)
+            acc = psum.tile([P, O], F32, name="acc")
+            nc.tensor.matmul_mx(acc[:], lhsT=ws_codes[:, cols].bitcast(E2M1), lhsT_scale=ws_plane[:, cols],
+                                rhs=x6_codes[:].bitcast(E5M2), rhs_scale=x6_plane[:], start=True, stop=False)
+            nc.tensor.matmul_mx(acc[:], lhsT=wb_codes[:, cols].bitcast(E2M1), lhsT_scale=wb_plane[:, cols],
+                                rhs=hid_codes[:].bitcast(E4M3), rhs_scale=hid_plane[:], start=False, stop=True)
+            y = keep.tile([P, O], F32, name="y%d" % half)
+            if half == 0:
+                nc.scalar.copy(y[:], acc[:])
+                nc.scalar.dma_start(out[cols, :], y[:])
+            else:
+                nc.vector.tensor_copy(y[:], acc[:])
+                nc.sync.dma_start(out[cols, :], y[:])

@@ -38,59 +38,63 @@ def tile_list_twogates_twow_further_plain_kernel(
             nc.sync.dma_start(tile[:], src)
             return tile
 
-        def load_plane(eng, plane, src):
+        def load_plane(eng, plane, src, quads=range(4)):
             rows = src[0].bitcast(I32)
-            for quad in range(4):
+            for quad in quads:
                 four = rows[4 * quad : 4 * quad + 4, :]
                 eng.dma_start(plane[32 * quad : 32 * quad + 32, :].bitcast(I32), four.unsqueeze(0).to_broadcast([8, 4, rows.shape[1]]))
+
+        def load_rows(eng, tile, src):
+            eng.dma_start(tile[:], src.rearrange("(p t) one -> p (t one)", t=PACK))
 
         xt_plane = keep.tile([P, T], U8, align_bytes=64)
         w_plane_raw = keep.tile([P, R], U8, align_bytes=64)
         w2_plane_raw = keep.tile([P, R], U8, align_bytes=64)
         wb_plane = keep.tile([P, N], U8, align_bytes=64)
         ws_plane = keep.tile([P, N], U8, align_bytes=64)
-
         sg_t = keep.tile([P, PACK], F32)
         bg_t = keep.tile([P, PACK], F32)
         sh_t = keep.tile([P, PACK], F32)
-        for tile, src in ((sg_t, sg), (bg_t, bg), (sh_t, sh)):
-            nc.gpsimd.dma_start(tile[:], src.rearrange("(p t) one -> p (t one)", t=PACK))
-
-        l1 = load_list(offs, "l1")
         xt_codes = keep.tile([P, T], U32, align_bytes=64)
-        nc.sync.dma_start(xt_codes[:].bitcast(I32), xt_words[0].rearrange("p c r -> p (c r)").bitcast(I32))
-        load_plane(nc.scalar, xt_plane, xt_scales)
-        l6 = load_list(offs6, "l6")
         tg_rows = tg.rearrange("(p t) q -> p t q", t=PACK)
         tg_t = [keep.tile([P, Q], F32, name="tg%d" % t) for t in range(PACK)]
-        nc.sync.dma_start(tg_t[0][:], tg_rows[:, 0, :])
-
-        l3 = load_list(offs3, "l3")
         w_raw = keep.tile([P, R], U16, align_bytes=64)
-        nc.sync.dma_start(w_raw[:].bitcast(I32), w_words[0].bitcast(I32))
-        load_plane(nc.sync, w_plane_raw, w_scales)
-        l5 = load_list(offs5, "l5")
-        nc.sync.dma_start(tg_t[1][:], tg_rows[:, 1, :])
-
-        l2 = load_list(offs2, "l2")
         w2_raw = keep.tile([P, R], U32, align_bytes=64)
+        ws_codes = keep.tile([P, N], U16, align_bytes=64)
+        wb_codes = keep.tile([P, N], U16, align_bytes=64)
+        l1 = load_list(offs, "l1")
+        load_plane(nc.scalar, xt_plane, xt_scales, range(3))
+        load_plane(nc.sync, xt_plane, xt_scales, range(3, 4))
+        l6 = load_list(offs6, "l6")
+        nc.sync.dma_start(w_raw[:].bitcast(I32), w_words[0].bitcast(I32))
+        nc.scalar.dma_start(xt_codes[:].bitcast(I32), xt_words[0].rearrange("p c r -> p (c r)").bitcast(I32))
+        load_plane(nc.sync, w_plane_raw, w_scales)
+        nc.sync.dma_start(tg_t[0][:], tg_rows[:, 0, :])
+        l3 = load_list(offs3, "l3")
+        load_rows(nc.sync, sg_t, sg)
+        load_rows(nc.sync, bg_t, bg)
+        l2 = load_list(offs2, "l2")
+        l5 = load_list(offs5, "l5")
+        load_rows(nc.sync, sh_t, sh)
+        nc.sync.dma_start(tg_t[1][:], tg_rows[:, 1, :])
         nc.sync.dma_start(w2_raw[:].bitcast(I32), w2_words[0].rearrange("p c r -> p (c r)").bitcast(I32))
         load_plane(nc.sync, w2_plane_raw, w2_scales)
         nc.sync.dma_start(tg_t[2][:], tg_rows[:, 2, :])
-        nc.sync.dma_start(tg_t[3][:], tg_rows[:, 3, :])
         l4 = load_list(offs4, "l4")
-        ws_codes = keep.tile([P, N], U16, align_bytes=64)
+        nc.sync.dma_start(tg_t[3][:], tg_rows[:, 3, :])
         nc.sync.dma_start(ws_codes[:].bitcast(I32), ws_words[0].bitcast(I32))
-        load_plane(nc.sync, ws_plane, ws_scales)
-        wb_codes = keep.tile([P, N], U16, align_bytes=64)
         nc.sync.dma_start(wb_codes[:].bitcast(I32), wb_words[0].bitcast(I32))
+        load_plane(nc.sync, ws_plane, ws_scales)
         load_plane(nc.sync, wb_plane, wb_scales)
 
         a_win = [keep.tile([P, J + SPARE], F32, name="a%d" % t) for t in range(PACK)]
         b_win = [keep.tile([P, J + SPARE], F32, name="b%d" % t) for t in range(PACK)]
-        for t in range(PACK):
-            nc.gpsimd.memset(a_win[t][:, J:], 0.0)
-            nc.gpsimd.memset(b_win[t][:, J:], 0.0)
+        for win in a_win + b_win:
+            nc.vector.memset(win[:, J:], 0.0)
+        warm_in = keep.tile([P, 1], F32)
+        warm_out = keep.tile([P, 1], F32)
+        nc.vector.memset(warm_in[:], 0.0)
+        nc.scalar.activation(warm_out[:], warm_in[:], SIGMOID)
 
         def dealt(raw):
             return raw[:].rearrange("p (m t) -> p t m", t=PACK)
@@ -99,19 +103,14 @@ def tile_list_twogates_twow_further_plain_kernel(
         nc.vector.tensor_copy(x1_plane[:], xt_plane[:].indirect(l1[:]))
         x1_codes = keep.tile([P, J], U32, align_bytes=64)
         nc.vector.tensor_copy(x1_codes[:], xt_codes[:].indirect(l1[:]))
-        x6_plane = keep.tile([P, O], U8, align_bytes=64)
-        nc.vector.tensor_copy(x6_plane[:], xt_plane[:].indirect(l6[:]))
-        x6_codes = keep.tile([P, O], U32, align_bytes=64)
-        nc.vector.tensor_copy(x6_codes[:], xt_codes[:].indirect(l6[:]))
         w_codes = keep.tile([P, PACK, P], U16, align_bytes=64)
         nc.scalar.copy(w_codes[:], dealt(w_raw))
         w_plane = keep.tile([P, PACK, P], U8, align_bytes=64)
         nc.vector.tensor_copy(w_plane[:], dealt(w_plane_raw))
-        w2_codes = keep.tile([P, PACK, P], U32, align_bytes=64)
-        nc.vector.tensor_copy(w2_codes[:], dealt(w2_raw))
-        w2_plane = keep.tile([P, PACK, P], U8, align_bytes=64)
-        nc.vector.tensor_copy(w2_plane[:], dealt(w2_plane_raw))
-
+        x6_plane = keep.tile([P, O], U8, align_bytes=64)
+        nc.vector.tensor_copy(x6_plane[:], xt_plane[:].indirect(l6[:]))
+        x6_codes = keep.tile([P, O], U32, align_bytes=64)
+        nc.vector.tensor_copy(x6_codes[:], xt_codes[:].indirect(l6[:]))
 
         def first_stage(codes, fmt, plane, t):
             acc = psum.tile([P, J], F32, name="acc")
@@ -119,20 +118,59 @@ def tile_list_twogates_twow_further_plain_kernel(
                                 rhs=x1_codes[:].bitcast(E5M2), rhs_scale=x1_plane[:], start=True, stop=True)
             return acc
 
-        a_acc = [first_stage(w_codes, E2M1, w_plane, t) for t in range(PACK)]
-        b_acc = [first_stage(w2_codes, E4M3, w2_plane, t) for t in range(PACK)]
-
         u1 = keep.tile([P, PACK, O], F32)
         u2 = keep.tile([P, PACK, O], F32)
-        for t in range(PACK):
-            g1 = keep.tile([P, O], F32, name="g1_%d" % t)
-            nc.scalar.activation(g1[:], tg_t[t][:].indirect(l3[:]), SIGMOID, bias=bg_t[:, t : t + 1], scale=sg_t[:, t : t + 1])
-            nc.vector.tensor_copy(a_win[t][:, :J], a_acc[t][:])
-            nc.vector.tensor_tensor(u1[:, t, :], a_win[t][:].indirect(l2[:]), g1[:], MULT)
-            g2 = keep.tile([P, O], F32, name="g2_%d" % t)
-            nc.scalar.activation(g2[:], tg_t[t][:].indirect(l5[:]), SIGMOID, scale=sh_t[:, t : t + 1])
-            nc.scalar.copy(b_win[t][:, :J], b_acc[t][:])
-            nc.vector.tensor_tensor(u2[:, t, :], b_win[t][:].indirect(l4[:]), g2[:], MULT)
+        g1 = [keep.tile([P, O], F32, name="g1_%d" % t) for t in range(PACK)]
+        g2 = [keep.tile([P, O], F32, name="g2_%d" % t) for t in range(PACK)]
+
+        def gate1(t):
+            nc.scalar.activation(g1[t][:], tg_t[t][:].indirect(l3[:]), SIGMOID, bias=bg_t[:, t : t + 1], scale=sg_t[:, t : t + 1])
+
+        def gate2(t):
+            nc.scalar.activation(g2[t][:], tg_t[t][:].indirect(l5[:]), SIGMOID, scale=sh_t[:, t : t + 1])
+
+        def prod1(t):
+            nc.vector.tensor_tensor(u1[:, t, :], a_win[t][:].indirect(l2[:]), g1[t][:], MULT)
+
+        def prod2(t):
+            nc.vector.tensor_tensor(u2[:, t, :], b_win[t][:].indirect(l4[:]), g2[t][:], MULT)
+
+        def out_v(win, acc):
+            nc.vector.tensor_copy(win[:, :J], acc[:])
+
+        def out_s(win, acc):
+            nc.scalar.copy(win[:, :J], acc[:])
+
+        a_acc = [first_stage(w_codes, E2M1, w_plane, t) for t in range(PACK)]
+        gate1(0)
+        out_v(a_win[0], a_acc[0])
+        out_v(a_win[1], a_acc[1])
+        gate2(0)
+        prod1(0)
+        out_v(a_win[2], a_acc[2])
+        gate1(1)
+        w2_codes = keep.tile([P, PACK, P], U32, align_bytes=64)
+        nc.scalar.copy(w2_codes[:], dealt(w2_raw))
+        w2_plane = keep.tile([P, PACK, P], U8, align_bytes=64)
+        nc.vector.tensor_copy(w2_plane[:], dealt(w2_plane_raw))
+        b_acc = [first_stage(w2_codes, E4M3, w2_plane, t) for t in range(PACK)]
+        gate2(1)
+        prod1(1)
+        out_s(b_win[0], b_acc[0])
+        out_s(b_win[1], b_acc[1])
+        gate1(2)
+        prod2(0)
+        prod2(1)
+        gate2(2)
+        out_s(b_win[2], b_acc[2])
+        prod1(2)
+        gate1(3)
+        out_s(a_win[3], a_acc[3])
+        prod2(2)
+        gate2(3)
+        out_s(b_win[3], b_acc[3])
+        prod1(3)
+        prod2(3)
 
         hid = keep.tile([P, O, PACK], BF16, align_bytes=64)
         nc.vector.tensor_tensor(

@@ -65,13 +65,13 @@ def tile_list_twogates_twow_further_plain_kernel(
         l1 = load_list(offs, "l1")
         load_plane(nc.scalar, xt_plane, xt_scales, range(3))
         load_plane(nc.sync, xt_plane, xt_scales, range(3, 4))
-        l6 = load_list(offs6, "l6")
+        load_rows(nc.sync, sg_t, sg)
         nc.sync.dma_start(w_raw[:].bitcast(I32), w_words[0].bitcast(I32))
         nc.scalar.dma_start(xt_codes[:].bitcast(I32), xt_words[0].rearrange("p c r -> p (c r)").bitcast(I32))
         load_plane(nc.sync, w_plane_raw, w_scales)
+        l6 = load_list(offs6, "l6")
         nc.sync.dma_start(tg_t[0][:], tg_rows[:, 0, :])
         l3 = load_list(offs3, "l3")
-        load_rows(nc.sync, sg_t, sg)
         load_rows(nc.sync, bg_t, bg)
         l2 = load_list(offs2, "l2")
         l5 = load_list(offs5, "l5")
@@ -147,53 +147,61 @@ def tile_list_twogates_twow_further_plain_kernel(
         out_v(a_win[1], a_acc[1])
         gate2(0)
         prod1(0)
-        out_v(a_win[2], a_acc[2])
         gate1(1)
+        out_v(a_win[2], a_acc[2])
         w2_codes = keep.tile([P, PACK, P], U32, align_bytes=64)
-        nc.scalar.copy(w2_codes[:], dealt(w2_raw))
+        nc.vector.tensor_copy(w2_codes[:], dealt(w2_raw))
         w2_plane = keep.tile([P, PACK, P], U8, align_bytes=64)
         nc.vector.tensor_copy(w2_plane[:], dealt(w2_plane_raw))
         b_acc = [first_stage(w2_codes, E4M3, w2_plane, t) for t in range(PACK)]
         gate2(1)
         prod1(1)
+        out_v(a_win[3], a_acc[3])
         out_s(b_win[0], b_acc[0])
-        out_s(b_win[1], b_acc[1])
         gate1(2)
         prod2(0)
-        prod2(1)
+        out_s(b_win[1], b_acc[1])
         gate2(2)
-        out_s(b_win[2], b_acc[2])
         prod1(2)
+        prod2(1)
+        out_s(b_win[2], b_acc[2])
         gate1(3)
-        out_s(a_win[3], a_acc[3])
+        out_s(b_win[3], b_acc[3])
         prod2(2)
         gate2(3)
-        out_s(b_win[3], b_acc[3])
         prod1(3)
         prod2(3)
 
-        hid = keep.tile([P, O, PACK], BF16, align_bytes=64)
-        nc.vector.tensor_tensor(
-            hid[:].rearrange("p (c i) t -> p c t i", i=4),
-            u1[:].rearrange("p t (c i) -> p c t i", i=4),
-            u2[:].rearrange("p t (c i) -> p c t i", i=4),
-            MAX,
-        )
-        hid_codes = keep.tile([P, O], U32, align_bytes=64)
-        hid_plane = keep.tile([P, O], U8, align_bytes=64)
-        nc.vector.quantize_mx(out=hid_codes[:].bitcast(E4M3), scales=hid_plane[:], in_=hid[:].rearrange("p o t -> p (o t)"))
+        halves = [slice(c * P, (c + 1) * P) for c in range(O // P)]
+        y_acc = {}
+        for c, places in enumerate(halves):
+            for h in range(N // P):
+                acc = psum.tile([P, P], F32, name="acc")
+                cols = slice(h * P, (h + 1) * P)
+                nc.tensor.matmul_mx(acc[:], lhsT=ws_codes[:, cols].bitcast(E2M1), lhsT_scale=ws_plane[:, cols],
+                                    rhs=x6_codes[:, places].bitcast(E5M2), rhs_scale=x6_plane[:, places], start=True, stop=False)
+                y_acc[c, h] = acc
 
-        for half in range(N // P):
-            cols = slice(half * P, (half + 1) * P)
-            acc = psum.tile([P, O], F32, name="acc")
-            nc.tensor.matmul_mx(acc[:], lhsT=ws_codes[:, cols].bitcast(E2M1), lhsT_scale=ws_plane[:, cols],
-                                rhs=x6_codes[:].bitcast(E5M2), rhs_scale=x6_plane[:], start=True, stop=False)
-            nc.tensor.matmul_mx(acc[:], lhsT=wb_codes[:, cols].bitcast(E2M1), lhsT_scale=wb_plane[:, cols],
-                                rhs=hid_codes[:].bitcast(E4M3), rhs_scale=hid_plane[:], start=False, stop=True)
-            y = keep.tile([P, O], F32, name="y%d" % half)
-            if half == 0:
-                nc.scalar.copy(y[:], acc[:])
-                nc.scalar.dma_start(out[cols, :], y[:])
-            else:
-                nc.vector.tensor_copy(y[:], acc[:])
-                nc.sync.dma_start(out[cols, :], y[:])
+        hid = [keep.tile([P, P, PACK], BF16, align_bytes=64, name="hid%d" % c) for c in range(O // P)]
+        for c, places in enumerate(halves):
+            nc.vector.tensor_tensor(
+                hid[c][:].rearrange("p (c i) t -> p c t i", i=4),
+                u1[:, :, places].rearrange("p t (c i) -> p c t i", i=4),
+                u2[:, :, places].rearrange("p t (c i) -> p c t i", i=4),
+                MAX,
+            )
+        y = [keep.tile([P, O], F32, name="y%d" % h) for h in range(N // P)]
+        for c, places in enumerate(halves):
+            hid_codes = keep.tile([P, P], U32, align_bytes=64, name="hid_codes%d" % c)
+            hid_plane = keep.tile([P, P], U8, align_bytes=64, name="hid_plane%d" % c)
+            nc.vector.quantize_mx(out=hid_codes[:].bitcast(E4M3), scales=hid_plane[:], in_=hid[c][:].rearrange("p o t -> p (o t)"))
+            for h in range(N // P):
+                cols = slice(h * P, (h + 1) * P)
+                nc.tensor.matmul_mx(y_acc[c, h][:], lhsT=wb_codes[:, cols].bitcast(E2M1), lhsT_scale=wb_plane[:, cols],
+                                    rhs=hid_codes[:].bitcast(E4M3), rhs_scale=hid_plane[:], start=False, stop=True)
+                if c == 1 and h == 1:
+                    nc.vector.tensor_copy(y[h][:, places], y_acc[c, h][:])
+                else:
+                    nc.scalar.copy(y[h][:, places], y_acc[c, h][:])
+        nc.scalar.dma_start(out[0:P, :], y[0][:])
+        nc.sync.dma_start(out[P:N, :], y[1][:])

@@ -48,7 +48,7 @@ def tile_list_twogates_twow_further_plain_kernel(
             eng.dma_start(tile[:], src.rearrange("(p t) one -> p (t one)", t=PACK))
 
         xt_plane = keep.tile([P, T], U8, align_bytes=64)
-        w_plane_raw = keep.tile([P, R], U8, align_bytes=64)
+        w_plane_raw = keep.tile([P, R], U8, align_bytes=64, tag="shared")
         w2_plane_raw = keep.tile([P, R], U8, align_bytes=64)
         wb_plane = keep.tile([P, N], U8, align_bytes=64)
         ws_plane = keep.tile([P, N], U8, align_bytes=64)
@@ -65,13 +65,13 @@ def tile_list_twogates_twow_further_plain_kernel(
         l1 = load_list(offs, "l1")
         load_plane(nc.scalar, xt_plane, xt_scales, range(3))
         load_plane(nc.sync, xt_plane, xt_scales, range(3, 4))
-        load_rows(nc.sync, sg_t, sg)
+        l6 = load_list(offs6, "l6")
         nc.sync.dma_start(w_raw[:].bitcast(I32), w_words[0].bitcast(I32))
         nc.scalar.dma_start(xt_codes[:].bitcast(I32), xt_words[0].rearrange("p c r -> p (c r)").bitcast(I32))
         load_plane(nc.sync, w_plane_raw, w_scales)
-        l6 = load_list(offs6, "l6")
         nc.sync.dma_start(tg_t[0][:], tg_rows[:, 0, :])
         l3 = load_list(offs3, "l3")
+        load_rows(nc.sync, sg_t, sg)
         load_rows(nc.sync, bg_t, bg)
         l2 = load_list(offs2, "l2")
         l5 = load_list(offs5, "l5")
@@ -109,7 +109,7 @@ def tile_list_twogates_twow_further_plain_kernel(
         nc.vector.tensor_copy(w_plane[:], dealt(w_plane_raw))
         x6_plane = keep.tile([P, O], U8, align_bytes=64)
         nc.vector.tensor_copy(x6_plane[:], xt_plane[:].indirect(l6[:]))
-        x6_codes = keep.tile([P, O], U32, align_bytes=64)
+        x6_codes = keep.tile([P, O], U32, align_bytes=64, tag="shared")
         nc.vector.tensor_copy(x6_codes[:], xt_codes[:].indirect(l6[:]))
 
         def first_stage(codes, fmt, plane, t):
@@ -145,10 +145,11 @@ def tile_list_twogates_twow_further_plain_kernel(
         gate1(0)
         out_v(a_win[0], a_acc[0])
         out_v(a_win[1], a_acc[1])
+        out_v(a_win[2], a_acc[2])
         gate2(0)
+        out_v(a_win[3], a_acc[3])
         prod1(0)
         gate1(1)
-        out_v(a_win[2], a_acc[2])
         w2_codes = keep.tile([P, PACK, P], U32, align_bytes=64)
         nc.vector.tensor_copy(w2_codes[:], dealt(w2_raw))
         w2_plane = keep.tile([P, PACK, P], U8, align_bytes=64)
@@ -156,7 +157,6 @@ def tile_list_twogates_twow_further_plain_kernel(
         b_acc = [first_stage(w2_codes, E4M3, w2_plane, t) for t in range(PACK)]
         gate2(1)
         prod1(1)
-        out_v(a_win[3], a_acc[3])
         out_s(b_win[0], b_acc[0])
         gate1(2)
         prod2(0)

from contextlib import ExitStack

import concourse.mybir as mybir

K, T, J, R, Q, O, N = 512, 1024, 256, 512, 1024, 256, 256
FLOPS = 2 * K * R * J * 2 + 2 * R * N * O + 2 * K * N * O

F32 = mybir.dt.float32
BF16 = mybir.dt.bfloat16
I32 = mybir.dt.int32
U32 = mybir.dt.uint32
U16 = mybir.dt.uint16
U8 = mybir.dt.uint8
E4M3 = mybir.dt.float8_e4m3fn_x4
E5M2 = mybir.dt.float8_e5m2_x4
E2M1 = mybir.dt.float4_e2m1fn_x4
MULT = mybir.AluOpType.mult
MAX = mybir.AluOpType.max
SIGMOID = mybir.ActivationFunctionType.Sigmoid

P = 128
PACK = 4
SPARE = 8


def tile_list_twogates_twow_further_plain_kernel(
    tc, xt_words, xt_scales, w_words, w_scales, w2_words, w2_scales, tg, sg, bg, sh,
    wb_words, wb_scales, ws_words, ws_scales, offs, offs2, offs3, offs4, offs5, offs6, out,
):
    nc = tc.nc
    with ExitStack() as ctx:
        lists = ctx.enter_context(tc.tile_pool(name="lists", bufs=1))
        keep = ctx.enter_context(tc.tile_pool(name="keep", bufs=1))
        psum = ctx.enter_context(tc.psum_pool(name="psum", bufs=8))

        def load_list(src, name):
            tile = lists.tile([P, 16], U16, name=name)
            nc.sync.dma_start(tile[:], src)
            return tile

        def load_plane(eng, plane, src, quads=range(4)):
            rows = src[0].bitcast(I32)
            for quad in quads:
                four = rows[4 * quad : 4 * quad + 4, :]
                eng.dma_start(plane[32 * quad : 32 * quad + 32, :].bitcast(I32), four.unsqueeze(0).to_broadcast([8, 4, rows.shape[1]]))

        def load_rows(eng, tile, src):
            eng.dma_start(tile[:], src.rearrange("(p t) one -> p (t one)", t=PACK))

        xt_plane = keep.tile([P, T], U8, align_bytes=64)
        w_plane_raw = keep.tile([P, R], U8, align_bytes=64, tag="shared")
        w2_plane_raw = keep.tile([P, R], U8, align_bytes=64)
        wb_plane = keep.tile([P, N], U8, align_bytes=64)
        ws_plane = keep.tile([P, N], U8, align_bytes=64)
        sg_t = keep.tile([P, PACK], F32)
        bg_t = keep.tile([P, PACK], F32)
        sh_t = keep.tile([P, PACK], F32)
        xt_codes = keep.tile([P, T], U32, align_bytes=64)
        tg_rows = tg.rearrange("(p t) q -> p t q", t=PACK)
        tg_t = [keep.tile([P, Q], F32, name="tg%d" % t) for t in range(PACK)]
        w_raw = keep.tile([P, R], U16, align_bytes=64)
        w2_raw = keep.tile([P, R], U32, align_bytes=64)
        ws_codes = keep.tile([P, N], U16, align_bytes=64)
        wb_codes = keep.tile([P, N], U16, align_bytes=64)
        l1 = load_list(offs, "l1")
        load_plane(nc.scalar, xt_plane, xt_scales, range(3))
        load_plane(nc.sync, xt_plane, xt_scales, range(3, 4))
        l6 = load_list(offs6, "l6")
        nc.sync.dma_start(w_raw[:].bitcast(I32), w_words[0].bitcast(I32))
        nc.scalar.dma_start(xt_codes[:].bitcast(I32), xt_words[0].rearrange("p c r -> p (c r)").bitcast(I32))
        load_plane(nc.sync, w_plane_raw, w_scales)
        nc.sync.dma_start(tg_t[0][:], tg_rows[:, 0, :])
        l3 = load_list(offs3, "l3")
        load_rows(nc.sync, sg_t, sg)
        load_rows(nc.sync, bg_t, bg)
        l2 = load_list(offs2, "l2")
        l5 = load_list(offs5, "l5")
        load_rows(nc.sync, sh_t, sh)
        nc.sync.dma_start(tg_t[1][:], tg_rows[:, 1, :])
        nc.sync.dma_start(w2_raw[:].bitcast(I32), w2_words[0].rearrange("p c r -> p (c r)").bitcast(I32))
        load_plane(nc.sync, w2_plane_raw, w2_scales)
        nc.sync.dma_start(tg_t[2][:], tg_rows[:, 2, :])
        l4 = load_list(offs4, "l4")
        nc.sync.dma_start(tg_t[3][:], tg_rows[:, 3, :])
        nc.sync.dma_start(ws_codes[:].bitcast(I32), ws_words[0].bitcast(I32))
        nc.sync.dma_start(wb_codes[:].bitcast(I32), wb_words[0].bitcast(I32))
        load_plane(nc.sync, ws_plane, ws_scales)
        load_plane(nc.sync, wb_plane, wb_scales)

        a_win = [keep.tile([P, J + SPARE], F32, name="a%d" % t) for t in range(PACK)]
        b_win = [keep.tile([P, J + SPARE], F32, name="b%d" % t) for t in range(PACK)]
        for win in a_win + b_win:
            nc.vector.memset(win[:, J:], 0.0)
        warm_in = keep.tile([P, 1], F32)
        warm_out = keep.tile([P, 1], F32)
        nc.vector.memset(warm_in[:], 0.0)
        nc.scalar.activation(warm_out[:], warm_in[:], SIGMOID)

        def dealt(raw):
            return raw[:].rearrange("p (m t) -> p t m", t=PACK)

        x1_plane = keep.tile([P, J], U8, align_bytes=64)
        nc.vector.tensor_copy(x1_plane[:], xt_plane[:].indirect(l1[:]))
        x1_codes = keep.tile([P, J], U32, align_bytes=64)
        nc.vector.tensor_copy(x1_codes[:], xt_codes[:].indirect(l1[:]))
        w_codes = keep.tile([P, PACK, P], U16, align_bytes=64)
        nc.scalar.copy(w_codes[:], dealt(w_raw))
        w_plane = keep.tile([P, PACK, P], U8, align_bytes=64)
        nc.vector.tensor_copy(w_plane[:], dealt(w_plane_raw))
        x6_plane = keep.tile([P, O], U8, align_bytes=64)
        nc.vector.tensor_copy(x6_plane[:], xt_plane[:].indirect(l6[:]))
        x6_codes = keep.tile([P, O], U32, align_bytes=64, tag="shared")
        nc.vector.tensor_copy(x6_codes[:], xt_codes[:].indirect(l6[:]))

        def first_stage(codes, fmt, plane, t):
            acc = psum.tile([P, J], F32, name="acc")
            nc.tensor.matmul_mx(acc[:], lhsT=codes[:, t, :].bitcast(fmt), lhsT_scale=plane[:, t, :],
                                rhs=x1_codes[:].bitcast(E5M2), rhs_scale=x1_plane[:], start=True, stop=True)
            return acc

        u1 = keep.tile([P, PACK, O], F32)
        u2 = keep.tile([P, PACK, O], F32)
        g1 = [keep.tile([P, O], F32, name="g1_%d" % t) for t in range(PACK)]
        g2 = [keep.tile([P, O], F32, name="g2_%d" % t) for t in range(PACK)]

        def gate1(t):
            nc.scalar.activation(g1[t][:], tg_t[t][:].indirect(l3[:]), SIGMOID, bias=bg_t[:, t : t + 1], scale=sg_t[:, t : t + 1])

        def gate2(t):
            nc.scalar.activation(g2[t][:], tg_t[t][:].indirect(l5[:]), SIGMOID, scale=sh_t[:, t : t + 1])

        def prod1(t):
            nc.vector.tensor_tensor(u1[:, t, :], a_win[t][:].indirect(l2[:]), g1[t][:], MULT)

        def prod2(t):
            nc.vector.tensor_tensor(u2[:, t, :], b_win[t][:].indirect(l4[:]), g2[t][:], MULT)

        def out_v(win, acc):
            nc.vector.tensor_copy(win[:, :J], acc[:])

        def out_s(win, acc):
            nc.scalar.copy(win[:, :J], acc[:])

        a_acc = [first_stage(w_codes, E2M1, w_plane, t) for t in range(PACK)]
        gate1(0)
        out_v(a_win[0], a_acc[0])
        out_v(a_win[1], a_acc[1])
        out_v(a_win[2], a_acc[2])
        gate2(0)
        out_v(a_win[3], a_acc[3])
        prod1(0)
        gate1(1)
        w2_codes = keep.tile([P, PACK, P], U32, align_bytes=64)
        nc.vector.tensor_copy(w2_codes[:], dealt(w2_raw))
        w2_plane = keep.tile([P, PACK, P], U8, align_bytes=64)
        nc.vector.tensor_copy(w2_plane[:], dealt(w2_plane_raw))
        b_acc = [first_stage(w2_codes, E4M3, w2_plane, t) for t in range(PACK)]
        gate2(1)
        prod1(1)
        out_s(b_win[0], b_acc[0])
        gate1(2)
        prod2(0)
        out_s(b_win[1], b_acc[1])
        gate2(2)
        prod1(2)
        prod2(1)
        out_s(b_win[2], b_acc[2])
        gate1(3)
        out_s(b_win[3], b_acc[3])
        prod2(2)
        gate2(3)
        prod1(3)
        prod2(3)

        halves = [slice(c * P, (c + 1) * P) for c in range(O // P)]
        y_acc = {}
        for c, places in enumerate(halves):
            for h in range(N // P):
                acc = psum.tile([P, P], F32, name="acc")
                cols = slice(h * P, (h + 1) * P)
                nc.tensor.matmul_mx(acc[:], lhsT=ws_codes[:, cols].bitcast(E2M1), lhsT_scale=ws_plane[:, cols],
                                    rhs=x6_codes[:, places].bitcast(E5M2), rhs_scale=x6_plane[:, places], start=True, stop=False)
                y_acc[c, h] = acc

        hid = [keep.tile([P, P, PACK], BF16, align_bytes=64, name="hid%d" % c) for c in range(O // P)]
        for c, places in enumerate(halves):
            nc.vector.tensor_tensor(
                hid[c][:].rearrange("p (c i) t -> p c t i", i=4),
                u1[:, :, places].rearrange("p t (c i) -> p c t i", i=4),
                u2[:, :, places].rearrange("p t (c i) -> p c t i", i=4),
                MAX,
            )
        y = [keep.tile([P, O], F32, name="y%d" % h) for h in range(N // P)]
        for c, places in enumerate(halves):
            hid_codes = keep.tile([P, P], U32, align_bytes=64, name="hid_codes%d" % c)
            hid_plane = keep.tile([P, P], U8, align_bytes=64, name="hid_plane%d" % c)
            nc.vector.quantize_mx(out=hid_codes[:].bitcast(E4M3), scales=hid_plane[:], in_=hid[c][:].rearrange("p o t -> p (o t)"))
            for h in range(N // P):
                cols = slice(h * P, (h + 1) * P)
                nc.tensor.matmul_mx(y_acc[c, h][:], lhsT=wb_codes[:, cols].bitcast(E2M1), lhsT_scale=wb_plane[:, cols],
                                    rhs=hid_codes[:].bitcast(E4M3), rhs_scale=hid_plane[:], start=False, stop=True)
                if c == 1 and h == 1:
                    nc.vector.tensor_copy(y[h][:, places], y_acc[c, h][:])
                else:
                    nc.scalar.copy(y[h][:, places], y_acc[c, h][:])
        nc.scalar.dma_start(out[0:P, :], y[0][:])
        nc.sync.dma_start(out[P:N, :], y[1][:])
